import numpy as np
import ml_dtypes


def mxq(x, axis, fmt="e4m3"):
    dtype, down = {"e4m3": (ml_dtypes.float8_e4m3fn, 7), "e5m2": (ml_dtypes.float8_e5m2, 14)}[fmt]
    v = np.moveaxis(np.asarray(x, np.float32).astype(ml_dtypes.bfloat16).astype(np.float64), axis, -1)
    blocks = v.reshape(v.shape[:-1] + (-1, 32))
    amax = np.abs(blocks).max(-1, keepdims=True)
    byte = np.maximum(np.where(amax > 0, np.frexp(amax)[1] - 1 + 127, 0) - down, 1)
    scale = np.exp2(byte - 127.0)
    codes = (blocks / scale).astype(np.float32).astype(dtype).astype(np.float64)
    return np.moveaxis((codes * scale).reshape(v.shape), -1, axis)


WIDE = False


def mx_kscale(k):
    if not WIDE:
        return np.ones(k)
    levels = np.array([10, -10, 5, -5, 0])
    if k % 512:
        return np.exp2(np.random.permutation(np.resize(levels, k // 32))).repeat(32)
    a = np.empty((k // 512, 16))
    for p in range(k // 512):
        a[p, :8] = np.random.permutation(np.resize(levels, 8))
        for g in range(8):
            far = levels[np.abs(levels - a[p, g]) >= 10]
            a[p, g + 8] = far[np.random.randint(len(far))]
    return np.exp2(a.ravel()).repeat(32)


def f64(x):
    return np.asarray(x).astype(np.float64)


def striped(idx):
    return np.tile(idx.reshape(-1, 16).T, (8, 1)).astype(np.uint16)


def unstriped(offs):
    return offs[:16].T.reshape(-1).astype(np.int64)


E2M1 = np.array([0.0, 0.5, 1.0, 1.5, 2.0, 3.0, 4.0, 6.0, -0.0, -0.5, -1.0, -1.5, -2.0, -3.0, -4.0, -6.0])


def pack_weight(w, fmt):
    k, n = w.shape
    w = f64(np.asarray(w, np.float32).astype(ml_dtypes.bfloat16)).reshape(k // 32, 32, n)
    amax = np.abs(w).max(1)
    if fmt == "e4m3":
        byte = np.frexp(amax)[1] - 1 + 127 - 7
    else:
        mant, ex = np.frexp(amax / 6.0)
        byte = np.where(mant > 0.5, ex, ex - 1) + 127
    byte = np.clip(np.where(amax > 0, byte, 1), 1, 254)
    scaled = (w * np.exp2(127.0 - byte)[:, None, :]).reshape(k, n).astype(np.float32)
    by_word = np.ascontiguousarray(scaled.reshape(k // 512, 128, 4, n).transpose(0, 1, 3, 2))
    if fmt == "e4m3":
        words = by_word.astype(ml_dtypes.float8_e4m3fn).view(np.uint8)
    else:
        c = by_word.astype(ml_dtypes.float4_e2m1fn).view(np.uint8) & 0xF
        words = (c[..., 0::2] | (c[..., 1::2] << 4)).reshape(k // 512, 128, 2 * n)
    return np.ascontiguousarray(words), np.ascontiguousarray(byte.astype(np.uint8).reshape(k // 512, 16, n))


def unpack_weight(words, scales, fmt):
    g, _, n = scales.shape
    words = np.ascontiguousarray(words).reshape(g, 128, n, -1)
    if fmt == "e4m3":
        vals = words.view(ml_dtypes.float8_e4m3fn).astype(np.float64)
    else:
        nib = np.empty((g, 128, n, 4), np.uint8)
        nib[..., 0::2] = words & 0xF
        nib[..., 1::2] = words >> 4
        vals = E2M1[nib]
    vals = vals * np.repeat(np.exp2(scales.astype(np.float64) - 127.0), 8, axis=1)[..., None]
    return vals.transpose(0, 1, 3, 2).reshape(g * 512, n)


def gelu(v):
    return 0.5 * v * (1.0 + np.tanh(np.sqrt(2.0 / np.pi) * (v + 0.044715 * v**3)))


K, H, N, T, S, T2, P = 1024, 1024, 384, 4096, 1024, 2048, 512

def setup_inputs():
    n = np.random.standard_normal
    s, u = mx_kscale(K)[:, None], mx_kscale(H)[:, None]
    tab_words, tab_scales = pack_weight(n((K, T)) * s, "e4m3")
    w2_words, w2_scales = pack_weight(n((H, N)) / np.sqrt(H) / u, "e2m1")
    perm = np.random.permutation(T2)
    return {
        "tab_words": tab_words, "tab_scales": tab_scales,
        "offs": striped(np.random.permutation(T)[:S]),
        "w1": (n((K, H)) / np.sqrt(K) / s).astype(np.float32),
        "level": n((H, S)).astype(np.float32),
        "gain": (np.exp(0.4 * n(H)) * u[:, 0]).astype(np.float32),
        "page0": (n((H, T2)) * u).astype(np.float32),
        "wgs": np.exp(0.3 * n((128, S))).astype(np.float32),
        "offs2": striped(np.random.permutation(T2)[:S]),
        "offs3": striped(perm[:P]), "offs4": striped(perm[P:2 * P]),
        "cross": (0.9 * n(H)).astype(np.float32),
        "w2_words": w2_words, "w2_scales": w2_scales,
        "w3": (n((H, N)) / np.sqrt(H) / u).astype(np.float32),
        "bias": (0.8 * n(N)).astype(np.float32),
    }

def reference(tab_words, tab_scales, offs, w1, level, gain, page0, wgs, offs2, offs3, offs4, cross, w2_words, w2_scales, w3, bias):
    v = unpack_weight(tab_words, tab_scales, "e4m3")[:, unstriped(offs)]
    y1 = mxq(f64(w1), 0, "e4m3").T @ v
    h = f64(gain)[:, None] * np.maximum(y1, f64(level))
    page = f64(page0).copy()
    page[:, unstriped(offs2)] = np.tile(f64(wgs), (H // 128, 1)) * h
    a = page[:, unstriped(offs3)]
    b = page[:, unstriped(offs4)]
    page[:, unstriped(offs3)] = a + b
    page[:, unstriped(offs4)] = a + f64(cross)[:, None] * b
    x = mxq(page, 0, "e4m3")
    y2 = unpack_weight(w2_words, w2_scales, "e2m1").T @ x
    y3 = mxq(f64(w3), 0, "e4m3").T @ x
    return np.maximum(y2, y3 + f64(bias)[:, None])

@@ -1,0 +1,341 @@
+from contextlib import ExitStack
+
+import concourse.mybir as mybir
+
+K, H, N, T, S, T2, PAIRS = 1024, 1024, 384, 4096, 1024, 2048, 512
+FLOPS = 2 * K * H * S + 2 * 2 * H * N * T2
+
+F32 = mybir.dt.float32
+BF16 = mybir.dt.bfloat16
+I32 = mybir.dt.int32
+U32 = mybir.dt.uint32
+U16 = mybir.dt.uint16
+U8 = mybir.dt.uint8
+FP8X4 = mybir.dt.float8_e4m3fn_x4
+FP4X4 = mybir.dt.float4_e2m1fn_x4
+MULT = mybir.AluOpType.mult
+ADD = mybir.AluOpType.add
+MAX = mybir.AluOpType.max
+COPY = mybir.ActivationFunctionType.Copy
+IDENTITY = mybir.ActivationFunctionType.Identity
+
+P = 128
+PACK = 4
+PASS = P * PACK
+BANK = 512
+SLICES = H // P
+CHUNKS = T2 // BANK
+LEAD = 320
+
+
+def tile_list_kerb_demand_scores_kernel(
+    tc, tab_words, tab_scales, offs, w1, level, gain, page0, wgs, offs2, offs3, offs4,
+    cross, w2_words, w2_scales, w3, bias, out,
+):
+    nc = tc.nc
+    with ExitStack() as ctx:
+        lists = ctx.enter_context(tc.tile_pool(name="lists", bufs=1))
+        keep = ctx.enter_context(tc.tile_pool(name="keep", bufs=1))
+        ring2 = ctx.enter_context(tc.tile_pool(name="ring2", bufs=2))
+        ring3 = ctx.enter_context(tc.tile_pool(name="ring3", bufs=3))
+        ring4 = ctx.enter_context(tc.tile_pool(name="ring4", bufs=4))
+        psum = ctx.enter_context(tc.psum_pool(name="psum", bufs=1))
+
+        idx = lists.tile([P, S // 16], U16, name="idx")
+        idx2 = lists.tile([P, S // 16], U16, name="idx2")
+        idx3 = lists.tile([P, PAIRS // 16], U16, name="idx3")
+        idx4 = lists.tile([P, PAIRS // 16], U16, name="idx4")
+
+        level_rows = level.rearrange("(b p t) j -> b t p j", p=P, t=PACK)
+        page_rows = page0.rearrange("(b p t) c -> b t p c", p=P, t=PACK)
+        wgs_rows = wgs.rearrange("(q t) j -> q t j", t=PACK)
+
+        def bank(i):
+            return psum.tile([P, BANK], F32, name="bank%d" % i, tag="bank%d" % i)
+
+        def load_words(a):
+            words = keep.tile([P, T], U32, name="words%d" % a, tag="big%d" % a, align_bytes=64)
+            nc.sync.dma_start(words[:].bitcast(I32), tab_words[a].rearrange("p t i -> p (t i)").bitcast(I32))
+            return words
+
+        def load_raw(w, a, c0, width):
+            raw = ring2.tile([P, PACK, width], F32, name="raw", tag="raw")
+            rows = w[a * PASS : (a + 1) * PASS, c0 : c0 + width]
+            nc.sync.dma_start(raw[:], rows.rearrange("(p j) c -> p j c", j=PACK))
+            return raw
+
+        def quantize(grouped, width, name):
+            codes = keep.tile([P, width], U32, name=name + "_codes", align_bytes=64)
+            scales = keep.tile([P, width], U8, name=name + "_scales", align_bytes=64)
+            nc.vector.quantize_mx(out=codes[:].bitcast(FP8X4), scales=scales[:], in_=grouped)
+            return codes, scales
+
+        def prepare_w1(raw, a, b):
+            grouped = ring2.tile([P, PASS * PACK], BF16, name="grouped", tag="grouped", align_bytes=64)
+            nc.scalar.copy(
+                grouped[:].rearrange("p (t m j) -> p m j t", t=PACK, j=PACK),
+                raw[:].rearrange("p j (m t) -> p m j t", t=PACK),
+            )
+            return quantize(grouped[:], PASS, "w1_%d%d" % (a, b))
+
+        def prepare_w3(raw, a):
+            grouped = ring2.tile([P, N * PACK], BF16, name="grouped", tag="grouped", align_bytes=64)
+            nc.scalar.copy(
+                grouped[:].rearrange("p (c i j) -> p c j i", i=PACK, j=PACK),
+                raw.rearrange("p j (c i) -> p c j i", i=PACK),
+            )
+            return quantize(grouped[:], N, "w3_%d" % a)
+
+        def load_wgs(t0, t1, j0, j1):
+            for q in range(4):
+                nc.sync.dma_start(wgs_sb[32 * q : 32 * q + 32, t0:t1, j0:j1], wgs_rows[:, t0:t1, j0:j1])
+
+        def load_page(s):
+            page = ring4.tile([P, T2], F32, name="page", tag="page")
+            nc.sync.dma_start(page[:], page_rows[s // PACK, s % PACK])
+            return page
+
+        def load_level(s):
+            lev = ring3.tile([P, S], F32, name="lev", tag="lev")
+            nc.sync.dma_start(lev[:], level_rows[s // PACK, s % PACK])
+            return lev
+
+        tab_plane = keep.tile([P, T], U8, name="tab_plane", align_bytes=64)
+        nc.vector.memset(tab_plane[:].bitcast(I32), 0)
+        w2_plane = keep.tile([P, 2, N], U8, name="w2_plane", align_bytes=64)
+        nc.vector.memset(w2_plane[:].rearrange("p a n -> p (a n)").bitcast(I32), 0)
+        for q in range(4):
+            nc.scalar.dma_start(
+                tab_plane[32 * q : 32 * q + 8, :].bitcast(I32), tab_scales[:, 4 * q : 4 * q + 4, :].bitcast(I32)
+            )
+        gain_sb = keep.tile([P, 2, 8], F32, name="gain_sb")
+        nc.scalar.dma_start(gain_sb[:, :, 0:PACK], gain.rearrange("(b p t) -> p b t", p=P, t=PACK))
+
+        wgs_sb = keep.tile([P, PACK, S], F32, name="wgs_sb")
+        words0 = load_words(0)
+        nc.sync.dma_start(idx[:], offs)
+        raw00 = load_raw(w1, 0, 0, PASS)
+        raw10 = load_raw(w1, 1, 0, PASS)
+        load_wgs(0, 1, 0, BANK)
+        words1 = load_words(1)
+        levels = {}
+        pages = {}
+        lev0 = ring3.tile([P, S], F32, name="lev", tag="lev")
+        levels[0] = lev0
+        nc.sync.dma_start(lev0[:, 0:BANK], level_rows[0, 0][:, 0:BANK])
+        pages[0] = load_page(0)
+        nc.sync.dma_start(idx2[:], offs2)
+        nc.sync.dma_start(lev0[:, BANK:S], level_rows[0, 0][:, BANK:S])
+        load_wgs(0, 1, BANK, S)
+        nc.sync.dma_start(idx3[:], offs3)
+        nc.sync.dma_start(idx4[:], offs4)
+        levels[1] = load_level(1)
+        load_wgs(1, 2, 0, S)
+        pages[1] = load_page(1)
+        cross_sb = keep.tile([P, 2, 8], F32, name="cross_sb")
+        nc.sync.dma_start(cross_sb[:, :, 0:PACK], cross.rearrange("(b p t) -> p b t", p=P, t=PACK))
+        load_wgs(2, 4, 0, S)
+
+        v_scales = keep.tile([P, S], U8, name="v_scales", align_bytes=64)
+        v_codes = [keep.tile([P, S], U32, name="v_codes%d" % a, align_bytes=64) for a in range(2)]
+        nc.vector.tensor_copy(v_scales[:], tab_plane[:].indirect(idx[:]))
+        nc.vector.tensor_copy(v_codes[0][:], words0[:].indirect(idx[:]))
+        w1q = {}
+        w1q[0, 0] = prepare_w1(raw00, 0, 0)
+        w1q[1, 0] = prepare_w1(raw10, 1, 0)
+        for half in range(2):
+            nc.vector.tensor_copy(
+                v_codes[1][:, half * BANK : (half + 1) * BANK],
+                words1[:].indirect(idx[:, half * 32 : (half + 1) * 32]),
+            )
+
+        held = keep.tile([P, S], F32, name="held")
+        weights = {}
+        firsts = {}
+        seconds = {}
+        crossed = {}
+
+        def weight(s, j0, j1):
+            nc.scalar.activation(
+                weights[s][:, j0:j1], wgs_sb[:, s % PACK, j0:j1], COPY,
+                scale=gain_sb[:, s // PACK, s % PACK : s % PACK + 1],
+            )
+
+        def first_product(s, half):
+            b, t = divmod(s, PACK)
+            cols = slice(half * BANK, (half + 1) * BANK)
+            acc = bank(4 + 2 * (s % 2) + half)
+            for a in range(2):
+                codes, scales = w1q[a, b]
+                nc.tensor.matmul_mx(
+                    out=acc[:],
+                    lhsT=codes[:, t * P : (t + 1) * P].bitcast(FP8X4),
+                    lhsT_scale=scales[:, t * P : (t + 1) * P],
+                    rhs=v_codes[a][:, cols].bitcast(FP8X4),
+                    rhs_scale=v_scales[4 * a : P, cols],
+                    start=(a == 0),
+                    stop=(a == 1),
+                )
+            nc.vector.tensor_tensor(held[:, cols], acc[:], levels[s][:, cols], MAX)
+
+        def write_records(s, j0, j1):
+            nc.vector.tensor_tensor(
+                pages[s][:].indirect(idx2[:, j0 // 16 : j1 // 16]), held[:, j0:j1], weights[s][:, j0:j1], MULT
+            )
+
+        def fetch_first(s):
+            firsts[s] = ring2.tile([P, PAIRS], F32, name="first", tag="first", align_bytes=64)
+            nc.vector.tensor_copy(firsts[s][:], pages[s][:].indirect(idx3[:]))
+
+        def fetch_second(s):
+            if s + 1 < SLICES:
+                seconds[s] = levels[s + 1][:, 0:PAIRS]
+            else:
+                spare = ring3.tile([P, S], F32, name="lev", tag="lev")
+                seconds[s] = spare[:, 0:PAIRS]
+            nc.vector.tensor_copy(seconds[s], pages[s][:].indirect(idx4[:]))
+            crossed[s] = ring2.tile([P, PAIRS], F32, name="crossed", tag="crossed", align_bytes=64)
+            nc.scalar.activation(
+                crossed[s][:], seconds[s], COPY, scale=cross_sb[:, s // PACK, s % PACK : s % PACK + 1]
+            )
+
+        def put_first(s):
+            nc.vector.tensor_tensor(pages[s][:].indirect(idx3[:]), firsts[s][:], seconds[s], ADD)
+
+        def put_second(s):
+            nc.vector.tensor_tensor(pages[s][:].indirect(idx4[:]), firsts[s][:], crossed[s][:], ADD)
+
+        x0 = keep.tile([P, T2, PACK], BF16, name="x0", tag="big0", align_bytes=64)
+        x1 = [keep.tile([P, BANK, PACK], BF16, name="x1_%d" % c, align_bytes=64) for c in range(CHUNKS)]
+
+        def round_page(s):
+            t = s % PACK
+            if s < PACK:
+                nc.scalar.copy(x0[:, :, t], pages[s][:])
+            else:
+                for c in range(CHUNKS):
+                    round_chunk(s, c)
+
+        def round_chunk(s, c):
+            t = s % PACK
+            c0 = LEAD if c == 0 and t >= 2 else 0
+            nc.scalar.copy(x1[c][:, c0:BANK, t], pages[s][:, c * BANK + c0 : (c + 1) * BANK])
+
+        def round_lead(s):
+            nc.vector.tensor_copy(x1[0][:, 0:LEAD, s % PACK], pages[s][:, 0:LEAD])
+
+        def quantize_x0(c):
+            tag = "first" if c % 2 == 0 else "crossed"
+            codes = ring2.tile([P, BANK], U32, name=tag, tag=tag, align_bytes=64)
+            cols = slice(c * BANK, (c + 1) * BANK)
+            nc.vector.quantize_mx(
+                out=codes[:].bitcast(FP8X4),
+                scales=x0_scales[c][:],
+                in_=x0[:, cols, :].rearrange("p c t -> p (c t)"),
+            )
+            xq[0, c] = (codes[:], x0_scales[c][:])
+
+        def quantize_x1(c):
+            codes, scales = quantize(x1[c][:].rearrange("p c t -> p (c t)"), BANK, "x1q_%d" % c)
+            xq[1, c] = (codes[:], scales[:])
+
+        x0_scales = [keep.tile([P, BANK], U8, name="x0_scales%d" % c, align_bytes=64) for c in range(CHUNKS)]
+        xq = {}
+
+        weights[0] = ring2.tile([P, S], F32, name="weight", tag="weight")
+        for half in range(2):
+            weight(0, half * BANK, (half + 1) * BANK)
+            first_product(0, half)
+            write_records(0, half * BANK, (half + 1) * BANK)
+        fetch_first(0)
+
+        w3q = {}
+        last = SLICES - 1
+        for s in range(1, SLICES):
+            weights[s] = ring2.tile([P, S], F32, name="weight", tag="weight")
+            weight(s, 0, S)
+            first_product(s, 0)
+            first_product(s, 1)
+            fetch_second(s - 1)
+            if s < last:
+                pages[s + 1] = load_page(s + 1)
+                levels[s + 1] = load_level(s + 1)
+            write_records(s, 0, S)
+            put_first(s - 1)
+            fetch_first(s)
+            if s == last:
+                fetch_second(s)
+            put_second(s - 1)
+            round_page(s - 1)
+            if s == 1:
+                for a in range(2):
+                    w1q[a, 1] = prepare_w1(load_raw(w1, a, PASS, PASS), a, 1)
+            if s == 2:
+                w3_raw = keep.tile([P, 2, PACK, N], F32, name="w3_raw", tag="big1", align_bytes=64)
+                nc.sync.dma_start(
+                    w3_raw[:].rearrange("p a j c -> p a (j c)"),
+                    w3.rearrange("(a p j) c -> p a (j c)", p=P, j=PACK),
+                )
+                for a in range(2):
+                    w3q[a] = prepare_w3(w3_raw[:, a], a)
+                w2_codes = keep.tile([P, 2, 2 * N], U8, name="w2_codes", align_bytes=64)
+                nc.sync.dma_start(
+                    w2_codes[:].bitcast(I32), w2_words.rearrange("a p c -> p a c").bitcast(I32)
+                )
+                for q in range(4):
+                    nc.sync.dma_start(
+                        w2_plane[32 * q : 32 * q + 4, :, :].bitcast(I32),
+                        w2_scales[:, 4 * q : 4 * q + 4, :].rearrange("a r n -> r a n").bitcast(I32),
+                    )
+                bias_sb = keep.tile([P, N // P], F32, name="bias_sb")
+                with nc.allow_non_contiguous_dma(reason="one bias value for each partition"):
+                    nc.sync.dma_start(bias_sb[:], bias.rearrange("(c p) -> p c", p=P))
+
+        put_first(last)
+        round_lead(last - 1)
+        quantize_x0(0)
+        quantize_x0(1)
+        put_second(last)
+
+        round_lead(last)
+        round_chunk(last, 0)
+        quantize_x1(0)
+        round_chunk(last, 1)
+        quantize_x1(1)
+        group = 0
+        for c in range(CHUNKS):
+            cols = slice(c * BANK, (c + 1) * BANK)
+            for n in range(N // P):
+                if n == 1 and c + 2 < CHUNKS:
+                    round_chunk(last, c + 2)
+                    quantize_x0(c + 2)
+                    quantize_x1(c + 2)
+                rows = slice(n * P, (n + 1) * P)
+                acc3 = bank(group % 8)
+                acc2 = bank((group + 1) % 8)
+                group = group + 2
+                for a in range(2):
+                    nc.tensor.matmul_mx(
+                        out=acc3[:],
+                        lhsT=w3q[a][0][:, rows].bitcast(FP8X4),
+                        lhsT_scale=w3q[a][1][:, rows],
+                        rhs=xq[a, c][0].bitcast(FP8X4),
+                        rhs_scale=xq[a, c][1],
+                        start=(a == 0),
+                        stop=(a == 1),
+                    )
+                for a in range(2):
+                    nc.tensor.matmul_mx(
+                        out=acc2[:],
+                        lhsT=w2_codes[:, a, 2 * n * P : 2 * (n + 1) * P].bitcast(FP4X4),
+                        lhsT_scale=w2_plane[:, a, rows],
+                        rhs=xq[a, c][0].bitcast(FP8X4),
+                        rhs_scale=xq[a, c][1],
+                        start=(a == 0),
+                        stop=(a == 1),
+                    )
+                shifted = ring3.tile([P, BANK], F32, name="shifted", tag="shifted")
+                nc.scalar.activation(shifted[:], acc3[:], IDENTITY, bias=bias_sb[:, n : n + 1])
+                score = ring4.tile([P, BANK], F32, name="score", tag="score")
+                nc.vector.tensor_tensor(score[:], acc2[:], shifted[:], MAX)
+                nc.sync.dma_start(out[rows, cols], score[:])

@@ -25,7 +25,7 @@ PASS = P * PACK
 BANK = 512
 SLICES = H // P
 CHUNKS = T2 // BANK
-LEAD = 320
+LEAD = 256
 
 
 def tile_list_kerb_demand_scores_kernel(
@@ -70,25 +70,29 @@ def tile_list_kerb_demand_scores_kernel(
             nc.vector.quantize_mx(out=codes[:].bitcast(FP8X4), scales=scales[:], in_=grouped)
             return codes, scales
 
-        def prepare_w1(raw, a, b):
-            grouped = ring2.tile([P, PASS * PACK], BF16, name="grouped", tag="grouped", align_bytes=64)
-            nc.scalar.copy(
-                grouped[:].rearrange("p (t m j) -> p m j t", t=PACK, j=PACK),
-                raw[:].rearrange("p j (m t) -> p m j t", t=PACK),
-            )
-            return quantize(grouped[:], PASS, "w1_%d%d" % (a, b))
+        def prepare_w1(raw, grouped, a, b):
+            if (a, b) == (1, 0):
+                nc.vector.tensor_copy(
+                    grouped.rearrange("p (t m j) -> p m t j", t=PACK, j=PACK),
+                    raw.rearrange("p j (m t) -> p m t j", t=PACK),
+                )
+            else:
+                nc.scalar.copy(
+                    grouped.rearrange("p (t m j) -> p m j t", t=PACK, j=PACK),
+                    raw.rearrange("p j (m t) -> p m j t", t=PACK),
+                )
+            return quantize(grouped, PASS, "w1_%d%d" % (a, b))
 
-        def prepare_w3(raw, a):
-            grouped = ring2.tile([P, N * PACK], BF16, name="grouped", tag="grouped", align_bytes=64)
+        def prepare_w3(raw, grouped, a):
             nc.scalar.copy(
-                grouped[:].rearrange("p (c i j) -> p c j i", i=PACK, j=PACK),
+                grouped.rearrange("p (c i j) -> p c j i", i=PACK, j=PACK),
                 raw.rearrange("p j (c i) -> p c j i", i=PACK),
             )
-            return quantize(grouped[:], N, "w3_%d" % a)
+            return quantize(grouped, N, "w3_%d" % a)
 
-        def load_wgs(t0, t1, j0, j1):
-            for q in range(4):
-                nc.sync.dma_start(wgs_sb[32 * q : 32 * q + 32, t0:t1, j0:j1], wgs_rows[:, t0:t1, j0:j1])
+        def load_wgs(t0, t1):
+            for q in (0, 2, 1, 3):
+                nc.sync.dma_start(wgs_sb[32 * q : 32 * q + 32, t0:t1, :], wgs_rows[:, t0:t1, :])
 
         def load_page(s):
             page = ring4.tile([P, T2], F32, name="page", tag="page")
@@ -105,44 +109,42 @@ def tile_list_kerb_demand_scores_kernel(
         w2_plane = keep.tile([P, 2, N], U8, name="w2_plane", align_bytes=64)
         nc.vector.memset(w2_plane[:].rearrange("p a n -> p (a n)").bitcast(I32), 0)
         for q in range(4):
-            nc.scalar.dma_start(
+            nc.gpsimd.dma_start(
                 tab_plane[32 * q : 32 * q + 8, :].bitcast(I32), tab_scales[:, 4 * q : 4 * q + 4, :].bitcast(I32)
             )
         gain_sb = keep.tile([P, 2, 8], F32, name="gain_sb")
-        nc.scalar.dma_start(gain_sb[:, :, 0:PACK], gain.rearrange("(b p t) -> p b t", p=P, t=PACK))
+        nc.gpsimd.dma_start(gain_sb[:, :, 0:PACK], gain.rearrange("(b p t) -> p b t", p=P, t=PACK))
 
         wgs_sb = keep.tile([P, PACK, S], F32, name="wgs_sb")
-        words0 = load_words(0)
         nc.sync.dma_start(idx[:], offs)
+        words0 = load_words(0)
         raw00 = load_raw(w1, 0, 0, PASS)
         raw10 = load_raw(w1, 1, 0, PASS)
-        load_wgs(0, 1, 0, BANK)
         words1 = load_words(1)
         levels = {}
         pages = {}
-        lev0 = ring3.tile([P, S], F32, name="lev", tag="lev")
-        levels[0] = lev0
-        nc.sync.dma_start(lev0[:, 0:BANK], level_rows[0, 0][:, 0:BANK])
+        levels[0] = load_level(0)
+        load_wgs(0, 1)
         pages[0] = load_page(0)
         nc.sync.dma_start(idx2[:], offs2)
-        nc.sync.dma_start(lev0[:, BANK:S], level_rows[0, 0][:, BANK:S])
-        load_wgs(0, 1, BANK, S)
+        load_wgs(1, 2)
+        levels[1] = load_level(1)
+        pages[1] = load_page(1)
+        late_raw = [load_raw(w1, 0, PASS, PASS)]
+        load_wgs(2, 3)
         nc.sync.dma_start(idx3[:], offs3)
         nc.sync.dma_start(idx4[:], offs4)
-        levels[1] = load_level(1)
-        load_wgs(1, 2, 0, S)
-        pages[1] = load_page(1)
         cross_sb = keep.tile([P, 2, 8], F32, name="cross_sb")
         nc.sync.dma_start(cross_sb[:, :, 0:PACK], cross.rearrange("(b p t) -> p b t", p=P, t=PACK))
-        load_wgs(2, 4, 0, S)
 
         v_scales = keep.tile([P, S], U8, name="v_scales", align_bytes=64)
         v_codes = [keep.tile([P, S], U32, name="v_codes%d" % a, align_bytes=64) for a in range(2)]
         nc.vector.tensor_copy(v_scales[:], tab_plane[:].indirect(idx[:]))
         nc.vector.tensor_copy(v_codes[0][:], words0[:].indirect(idx[:]))
         w1q = {}
-        w1q[0, 0] = prepare_w1(raw00, 0, 0)
-        w1q[1, 0] = prepare_w1(raw10, 1, 0)
+        for a, raw in enumerate((raw00, raw10)):
+            grouped = ring2.tile([P, PASS * PACK], BF16, name="grouped", tag="grouped", align_bytes=64)
+            w1q[a, 0] = prepare_w1(raw[:], grouped[:], a, 0)
         for half in range(2):
             nc.vector.tensor_copy(
                 v_codes[1][:, half * BANK : (half + 1) * BANK],
@@ -155,9 +157,10 @@ def tile_list_kerb_demand_scores_kernel(
         seconds = {}
         crossed = {}
 
-        def weight(s, j0, j1):
+        def weight(s):
+            weights[s] = ring2.tile([P, S], F32, name="weight", tag="weight", align_bytes=64)
             nc.scalar.activation(
-                weights[s][:, j0:j1], wgs_sb[:, s % PACK, j0:j1], COPY,
+                weights[s][:], wgs_sb[:, s % PACK, :], COPY,
                 scale=gain_sb[:, s // PACK, s % PACK : s % PACK + 1],
             )
 
@@ -178,10 +181,8 @@ def tile_list_kerb_demand_scores_kernel(
                 )
             nc.vector.tensor_tensor(held[:, cols], acc[:], levels[s][:, cols], MAX)
 
-        def write_records(s, j0, j1):
-            nc.vector.tensor_tensor(
-                pages[s][:].indirect(idx2[:, j0 // 16 : j1 // 16]), held[:, j0:j1], weights[s][:, j0:j1], MULT
-            )
+        def write_records(s):
+            nc.vector.tensor_tensor(pages[s][:].indirect(idx2[:]), held[:], weights[s][:], MULT)
 
         def fetch_first(s):
             firsts[s] = ring2.tile([P, PAIRS], F32, name="first", tag="first", align_bytes=64)
@@ -225,8 +226,11 @@ def tile_list_kerb_demand_scores_kernel(
             nc.vector.tensor_copy(x1[0][:, 0:LEAD, s % PACK], pages[s][:, 0:LEAD])
 
         def quantize_x0(c):
-            tag = "first" if c % 2 == 0 else "crossed"
-            codes = ring2.tile([P, BANK], U32, name=tag, tag=tag, align_bytes=64)
+            if c < 2:
+                codes = ring2.tile([P, BANK], U32, name="first", tag="first", align_bytes=64)
+            else:
+                tag = "early%d" % (c - 2)
+                codes = keep.tile([P, BANK], U32, name=tag, tag=tag, align_bytes=64)
             cols = slice(c * BANK, (c + 1) * BANK)
             nc.vector.quantize_mx(
                 out=codes[:].bitcast(FP8X4),
@@ -242,42 +246,45 @@ def tile_list_kerb_demand_scores_kernel(
         x0_scales = [keep.tile([P, BANK], U8, name="x0_scales%d" % c, align_bytes=64) for c in range(CHUNKS)]
         xq = {}
 
-        weights[0] = ring2.tile([P, S], F32, name="weight", tag="weight")
-        for half in range(2):
-            weight(0, half * BANK, (half + 1) * BANK)
-            first_product(0, half)
-            write_records(0, half * BANK, (half + 1) * BANK)
+        weight(0)
+        first_product(0, 0)
+        first_product(0, 1)
+        write_records(0)
         fetch_first(0)
+        weight(1)
 
         w3q = {}
         last = SLICES - 1
         for s in range(1, SLICES):
-            weights[s] = ring2.tile([P, S], F32, name="weight", tag="weight")
-            weight(s, 0, S)
             first_product(s, 0)
             first_product(s, 1)
             fetch_second(s - 1)
+            if s == 1:
+                load_wgs(3, 4)
+                raw11 = keep.tile([P, PACK, PASS], F32, name="raw11", tag="big1", align_bytes=64)
+                nc.sync.dma_start(raw11[:], w1[PASS:K, PASS:H].rearrange("(p j) c -> p j c", j=PACK))
+                late_raw.append(raw11)
+            if s == 3:
+                w3_raw = [load_raw(w3, a, 0, N) for a in range(2)]
             if s < last:
                 pages[s + 1] = load_page(s + 1)
                 levels[s + 1] = load_level(s + 1)
-            write_records(s, 0, S)
+            if s < last:
+                weight(s + 1)
+            write_records(s)
             put_first(s - 1)
             fetch_first(s)
             if s == last:
                 fetch_second(s)
             put_second(s - 1)
             round_page(s - 1)
-            if s == 1:
-                for a in range(2):
-                    w1q[a, 1] = prepare_w1(load_raw(w1, a, PASS, PASS), a, 1)
-            if s == 2:
-                w3_raw = keep.tile([P, 2, PACK, N], F32, name="w3_raw", tag="big1", align_bytes=64)
-                nc.sync.dma_start(
-                    w3_raw[:].rearrange("p a j c -> p a (j c)"),
-                    w3.rearrange("(a p j) c -> p a (j c)", p=P, j=PACK),
-                )
-                for a in range(2):
-                    w3q[a] = prepare_w3(w3_raw[:, a], a)
+            if s in (1, 2):
+                late = ring2.tile([P, PASS * PACK], BF16, name="weight", tag="weight", align_bytes=64)
+                w1q[s - 1, 1] = prepare_w1(late_raw[s - 1][:], late[:], s - 1, 1)
+            if s in (4, 5):
+                late = ring2.tile([P, N * PACK], BF16, name="weight", tag="weight", align_bytes=64)
+                w3q[s - 4] = prepare_w3(w3_raw[s - 4][:], late[:], s - 4)
+            if s == 5:
                 w2_codes = keep.tile([P, 2, 2 * N], U8, name="w2_codes", align_bytes=64)
                 nc.sync.dma_start(
                     w2_codes[:].bitcast(I32), w2_words.rearrange("a p c -> p a c").bitcast(I32)
@@ -294,21 +301,21 @@ def tile_list_kerb_demand_scores_kernel(
         put_first(last)
         round_lead(last - 1)
         quantize_x0(0)
-        quantize_x0(1)
         put_second(last)
 
         round_lead(last)
         round_chunk(last, 0)
         quantize_x1(0)
+        quantize_x0(1)
         round_chunk(last, 1)
         quantize_x1(1)
         group = 0
         for c in range(CHUNKS):
             cols = slice(c * BANK, (c + 1) * BANK)
+            score = ring4.tile([P, N // P, BANK], F32, name="page", tag="page")
             for n in range(N // P):
                 if n == 1 and c + 2 < CHUNKS:
                     round_chunk(last, c + 2)
-                    quantize_x0(c + 2)
                     quantize_x1(c + 2)
                 rows = slice(n * P, (n + 1) * P)
                 acc3 = bank(group % 8)
@@ -334,8 +341,14 @@ def tile_list_kerb_demand_scores_kernel(
                         start=(a == 0),
                         stop=(a == 1),
                     )
-                shifted = ring3.tile([P, BANK], F32, name="shifted", tag="shifted")
-                nc.scalar.activation(shifted[:], acc3[:], IDENTITY, bias=bias_sb[:, n : n + 1])
-                score = ring4.tile([P, BANK], F32, name="score", tag="score")
-                nc.vector.tensor_tensor(score[:], acc2[:], shifted[:], MAX)
-                nc.sync.dma_start(out[rows, cols], score[:])
+                early = c == 0 and n < 2
+                if early:
+                    shifted = keep.tile([P, BANK], F32, name="early%d" % n, tag="early%d" % n, align_bytes=64)
+                    nc.vector.tensor_scalar(shifted[:], acc3[:], bias_sb[:, n : n + 1], None, ADD)
+                else:
+                    shifted = ring3.tile([P, BANK], F32, name="shifted", tag="shifted")
+                    nc.scalar.activation(shifted[:], acc3[:], IDENTITY, bias=bias_sb[:, n : n + 1])
+                nc.vector.tensor_tensor(score[:, n], acc2[:], shifted[:], MAX)
+                nc.sync.dma_start(out[rows, cols], score[:, n])
+                if early:
+                    quantize_x0(n + 2)

from contextlib import ExitStack

import concourse.mybir as mybir

K, H, N, T, S, T2, PAIRS = 1024, 1024, 384, 4096, 1024, 2048, 512
FLOPS = 2 * K * H * S + 2 * 2 * H * N * T2

F32 = mybir.dt.float32
BF16 = mybir.dt.bfloat16
I32 = mybir.dt.int32
U32 = mybir.dt.uint32
U16 = mybir.dt.uint16
U8 = mybir.dt.uint8
FP8X4 = mybir.dt.float8_e4m3fn_x4
FP4X4 = mybir.dt.float4_e2m1fn_x4
MULT = mybir.AluOpType.mult
ADD = mybir.AluOpType.add
MAX = mybir.AluOpType.max
COPY = mybir.ActivationFunctionType.Copy
IDENTITY = mybir.ActivationFunctionType.Identity

P = 128
PACK = 4
PASS = P * PACK
BANK = 512
SLICES = H // P
CHUNKS = T2 // BANK
LEAD = 256


def tile_list_kerb_demand_scores_kernel(
    tc, tab_words, tab_scales, offs, w1, level, gain, page0, wgs, offs2, offs3, offs4,
    cross, w2_words, w2_scales, w3, bias, out,
):
    nc = tc.nc
    with ExitStack() as ctx:
        lists = ctx.enter_context(tc.tile_pool(name="lists", bufs=1))
        keep = ctx.enter_context(tc.tile_pool(name="keep", bufs=1))
        ring2 = ctx.enter_context(tc.tile_pool(name="ring2", bufs=2))
        ring3 = ctx.enter_context(tc.tile_pool(name="ring3", bufs=3))
        ring4 = ctx.enter_context(tc.tile_pool(name="ring4", bufs=4))
        psum = ctx.enter_context(tc.psum_pool(name="psum", bufs=1))

        idx = lists.tile([P, S // 16], U16, name="idx")
        idx2 = lists.tile([P, S // 16], U16, name="idx2")
        idx3 = lists.tile([P, PAIRS // 16], U16, name="idx3")
        idx4 = lists.tile([P, PAIRS // 16], U16, name="idx4")

        level_rows = level.rearrange("(b p t) j -> b t p j", p=P, t=PACK)
        page_rows = page0.rearrange("(b p t) c -> b t p c", p=P, t=PACK)
        wgs_rows = wgs.rearrange("(q t) j -> q t j", t=PACK)

        def bank(i):
            return psum.tile([P, BANK], F32, name="bank%d" % i, tag="bank%d" % i)

        def load_words(a):
            words = keep.tile([P, T], U32, name="words%d" % a, tag="big%d" % a, align_bytes=64)
            nc.sync.dma_start(words[:].bitcast(I32), tab_words[a].rearrange("p t i -> p (t i)").bitcast(I32))
            return words

        def load_raw(w, a, c0, width):
            raw = ring2.tile([P, PACK, width], F32, name="raw", tag="raw")
            rows = w[a * PASS : (a + 1) * PASS, c0 : c0 + width]
            nc.sync.dma_start(raw[:], rows.rearrange("(p j) c -> p j c", j=PACK))
            return raw

        def quantize(grouped, width, name):
            codes = keep.tile([P, width], U32, name=name + "_codes", align_bytes=64)
            scales = keep.tile([P, width], U8, name=name + "_scales", align_bytes=64)
            nc.vector.quantize_mx(out=codes[:].bitcast(FP8X4), scales=scales[:], in_=grouped)
            return codes, scales

        def prepare_w1(raw, grouped, a, b):
            if (a, b) == (1, 0):
                nc.vector.tensor_copy(
                    grouped.rearrange("p (t m j) -> p m t j", t=PACK, j=PACK),
                    raw.rearrange("p j (m t) -> p m t j", t=PACK),
                )
            else:
                nc.scalar.copy(
                    grouped.rearrange("p (t m j) -> p m j t", t=PACK, j=PACK),
                    raw.rearrange("p j (m t) -> p m j t", t=PACK),
                )
            return quantize(grouped, PASS, "w1_%d%d" % (a, b))

        def prepare_w3(raw, grouped, a):
            nc.scalar.copy(
                grouped.rearrange("p (c i j) -> p c j i", i=PACK, j=PACK),
                raw.rearrange("p j (c i) -> p c j i", i=PACK),
            )
            return quantize(grouped, N, "w3_%d" % a)

        def load_wgs(t0, t1):
            for q in (0, 2, 1, 3):
                nc.sync.dma_start(wgs_sb[32 * q : 32 * q + 32, t0:t1, :], wgs_rows[:, t0:t1, :])

        def load_page(s):
            page = ring4.tile([P, T2], F32, name="page", tag="page")
            nc.sync.dma_start(page[:], page_rows[s // PACK, s % PACK])
            return page

        def load_level(s):
            lev = ring3.tile([P, S], F32, name="lev", tag="lev")
            nc.sync.dma_start(lev[:], level_rows[s // PACK, s % PACK])
            return lev

        tab_plane = keep.tile([P, T], U8, name="tab_plane", align_bytes=64)
        nc.vector.memset(tab_plane[:].bitcast(I32), 0)
        w2_plane = keep.tile([P, 2, N], U8, name="w2_plane", align_bytes=64)
        nc.vector.memset(w2_plane[:].rearrange("p a n -> p (a n)").bitcast(I32), 0)
        for q in range(4):
            nc.gpsimd.dma_start(
                tab_plane[32 * q : 32 * q + 8, :].bitcast(I32), tab_scales[:, 4 * q : 4 * q + 4, :].bitcast(I32)
            )
        gain_sb = keep.tile([P, 2, 8], F32, name="gain_sb")
        nc.gpsimd.dma_start(gain_sb[:, :, 0:PACK], gain.rearrange("(b p t) -> p b t", p=P, t=PACK))

        wgs_sb = keep.tile([P, PACK, S], F32, name="wgs_sb")
        nc.sync.dma_start(idx[:], offs)
        words0 = load_words(0)
        raw00 = load_raw(w1, 0, 0, PASS)
        raw10 = load_raw(w1, 1, 0, PASS)
        words1 = load_words(1)
        levels = {}
        pages = {}
        levels[0] = load_level(0)
        load_wgs(0, 1)
        pages[0] = load_page(0)
        nc.sync.dma_start(idx2[:], offs2)
        load_wgs(1, 2)
        levels[1] = load_level(1)
        pages[1] = load_page(1)
        late_raw = [load_raw(w1, 0, PASS, PASS)]
        load_wgs(2, 3)
        nc.sync.dma_start(idx3[:], offs3)
        nc.sync.dma_start(idx4[:], offs4)
        cross_sb = keep.tile([P, 2, 8], F32, name="cross_sb")
        nc.sync.dma_start(cross_sb[:, :, 0:PACK], cross.rearrange("(b p t) -> p b t", p=P, t=PACK))

        v_scales = keep.tile([P, S], U8, name="v_scales", align_bytes=64)
        v_codes = [keep.tile([P, S], U32, name="v_codes%d" % a, align_bytes=64) for a in range(2)]
        nc.vector.tensor_copy(v_scales[:], tab_plane[:].indirect(idx[:]))
        nc.vector.tensor_copy(v_codes[0][:], words0[:].indirect(idx[:]))
        w1q = {}
        for a, raw in enumerate((raw00, raw10)):
            grouped = ring2.tile([P, PASS * PACK], BF16, name="grouped", tag="grouped", align_bytes=64)
            w1q[a, 0] = prepare_w1(raw[:], grouped[:], a, 0)
        for half in range(2):
            nc.vector.tensor_copy(
                v_codes[1][:, half * BANK : (half + 1) * BANK],
                words1[:].indirect(idx[:, half * 32 : (half + 1) * 32]),
            )

        held = keep.tile([P, S], F32, name="held")
        weights = {}
        firsts = {}
        seconds = {}
        crossed = {}

        def weight(s):
            weights[s] = ring2.tile([P, S], F32, name="weight", tag="weight", align_bytes=64)
            nc.scalar.activation(
                weights[s][:], wgs_sb[:, s % PACK, :], COPY,
                scale=gain_sb[:, s // PACK, s % PACK : s % PACK + 1],
            )

        def first_product(s, half):
            b, t = divmod(s, PACK)
            cols = slice(half * BANK, (half + 1) * BANK)
            acc = bank(4 + 2 * (s % 2) + half)
            for a in range(2):
                codes, scales = w1q[a, b]
                nc.tensor.matmul_mx(
                    out=acc[:],
                    lhsT=codes[:, t * P : (t + 1) * P].bitcast(FP8X4),
                    lhsT_scale=scales[:, t * P : (t + 1) * P],
                    rhs=v_codes[a][:, cols].bitcast(FP8X4),
                    rhs_scale=v_scales[4 * a : P, cols],
                    start=(a == 0),
                    stop=(a == 1),
                )
            nc.vector.tensor_tensor(held[:, cols], acc[:], levels[s][:, cols], MAX)

        def write_records(s):
            nc.vector.tensor_tensor(pages[s][:].indirect(idx2[:]), held[:], weights[s][:], MULT)

        def fetch_first(s):
            firsts[s] = ring2.tile([P, PAIRS], F32, name="first", tag="first", align_bytes=64)
            nc.vector.tensor_copy(firsts[s][:], pages[s][:].indirect(idx3[:]))

        def fetch_second(s):
            if s + 1 < SLICES:
                seconds[s] = levels[s + 1][:, 0:PAIRS]
            else:
                spare = ring3.tile([P, S], F32, name="lev", tag="lev")
                seconds[s] = spare[:, 0:PAIRS]
            nc.vector.tensor_copy(seconds[s], pages[s][:].indirect(idx4[:]))
            crossed[s] = ring2.tile([P, PAIRS], F32, name="crossed", tag="crossed", align_bytes=64)
            nc.scalar.activation(
                crossed[s][:], seconds[s], COPY, scale=cross_sb[:, s // PACK, s % PACK : s % PACK + 1]
            )

        def put_first(s):
            nc.vector.tensor_tensor(pages[s][:].indirect(idx3[:]), firsts[s][:], seconds[s], ADD)

        def put_second(s):
            nc.vector.tensor_tensor(pages[s][:].indirect(idx4[:]), firsts[s][:], crossed[s][:], ADD)

        x0 = keep.tile([P, T2, PACK], BF16, name="x0", tag="big0", align_bytes=64)
        x1 = [keep.tile([P, BANK, PACK], BF16, name="x1_%d" % c, align_bytes=64) for c in range(CHUNKS)]

        def round_page(s):
            t = s % PACK
            if s < PACK:
                nc.scalar.copy(x0[:, :, t], pages[s][:])
            else:
                for c in range(CHUNKS):
                    round_chunk(s, c)

        def round_chunk(s, c):
            t = s % PACK
            c0 = LEAD if c == 0 and t >= 2 else 0
            nc.scalar.copy(x1[c][:, c0:BANK, t], pages[s][:, c * BANK + c0 : (c + 1) * BANK])

        def round_lead(s):
            nc.vector.tensor_copy(x1[0][:, 0:LEAD, s % PACK], pages[s][:, 0:LEAD])

        def quantize_x0(c):
            if c < 2:
                codes = ring2.tile([P, BANK], U32, name="first", tag="first", align_bytes=64)
            else:
                tag = "early%d" % (c - 2)
                codes = keep.tile([P, BANK], U32, name=tag, tag=tag, align_bytes=64)
            cols = slice(c * BANK, (c + 1) * BANK)
            nc.vector.quantize_mx(
                out=codes[:].bitcast(FP8X4),
                scales=x0_scales[c][:],
                in_=x0[:, cols, :].rearrange("p c t -> p (c t)"),
            )
            xq[0, c] = (codes[:], x0_scales[c][:])

        def quantize_x1(c):
            codes, scales = quantize(x1[c][:].rearrange("p c t -> p (c t)"), BANK, "x1q_%d" % c)
            xq[1, c] = (codes[:], scales[:])

        x0_scales = [keep.tile([P, BANK], U8, name="x0_scales%d" % c, align_bytes=64) for c in range(CHUNKS)]
        xq = {}

        weight(0)
        first_product(0, 0)
        first_product(0, 1)
        write_records(0)
        fetch_first(0)
        weight(1)

        w3q = {}
        last = SLICES - 1
        for s in range(1, SLICES):
            first_product(s, 0)
            first_product(s, 1)
            fetch_second(s - 1)
            if s == 1:
                load_wgs(3, 4)
                raw11 = keep.tile([P, PACK, PASS], F32, name="raw11", tag="big1", align_bytes=64)
                nc.sync.dma_start(raw11[:], w1[PASS:K, PASS:H].rearrange("(p j) c -> p j c", j=PACK))
                late_raw.append(raw11)
            if s == 3:
                w3_raw = [load_raw(w3, a, 0, N) for a in range(2)]
            if s < last:
                pages[s + 1] = load_page(s + 1)
                levels[s + 1] = load_level(s + 1)
            if s < last:
                weight(s + 1)
            write_records(s)
            put_first(s - 1)
            fetch_first(s)
            if s == last:
                fetch_second(s)
            put_second(s - 1)
            round_page(s - 1)
            if s in (1, 2):
                late = ring2.tile([P, PASS * PACK], BF16, name="weight", tag="weight", align_bytes=64)
                w1q[s - 1, 1] = prepare_w1(late_raw[s - 1][:], late[:], s - 1, 1)
            if s in (4, 5):
                late = ring2.tile([P, N * PACK], BF16, name="weight", tag="weight", align_bytes=64)
                w3q[s - 4] = prepare_w3(w3_raw[s - 4][:], late[:], s - 4)
            if s == 5:
                w2_codes = keep.tile([P, 2, 2 * N], U8, name="w2_codes", align_bytes=64)
                nc.sync.dma_start(
                    w2_codes[:].bitcast(I32), w2_words.rearrange("a p c -> p a c").bitcast(I32)
                )
                for q in range(4):
                    nc.sync.dma_start(
                        w2_plane[32 * q : 32 * q + 4, :, :].bitcast(I32),
                        w2_scales[:, 4 * q : 4 * q + 4, :].rearrange("a r n -> r a n").bitcast(I32),
                    )
                bias_sb = keep.tile([P, N // P], F32, name="bias_sb")
                with nc.allow_non_contiguous_dma(reason="one bias value for each partition"):
                    nc.sync.dma_start(bias_sb[:], bias.rearrange("(c p) -> p c", p=P))

        put_first(last)
        round_lead(last - 1)
        quantize_x0(0)
        put_second(last)

        round_lead(last)
        round_chunk(last, 0)
        quantize_x1(0)
        quantize_x0(1)
        round_chunk(last, 1)
        quantize_x1(1)
        group = 0
        for c in range(CHUNKS):
            cols = slice(c * BANK, (c + 1) * BANK)
            score = ring4.tile([P, N // P, BANK], F32, name="page", tag="page")
            for n in range(N // P):
                if n == 1 and c + 2 < CHUNKS:
                    round_chunk(last, c + 2)
                    quantize_x1(c + 2)
                rows = slice(n * P, (n + 1) * P)
                acc3 = bank(group % 8)
                acc2 = bank((group + 1) % 8)
                group = group + 2
                for a in range(2):
                    nc.tensor.matmul_mx(
                        out=acc3[:],
                        lhsT=w3q[a][0][:, rows].bitcast(FP8X4),
                        lhsT_scale=w3q[a][1][:, rows],
                        rhs=xq[a, c][0].bitcast(FP8X4),
                        rhs_scale=xq[a, c][1],
                        start=(a == 0),
                        stop=(a == 1),
                    )
                for a in range(2):
                    nc.tensor.matmul_mx(
                        out=acc2[:],
                        lhsT=w2_codes[:, a, 2 * n * P : 2 * (n + 1) * P].bitcast(FP4X4),
                        lhsT_scale=w2_plane[:, a, rows],
                        rhs=xq[a, c][0].bitcast(FP8X4),
                        rhs_scale=xq[a, c][1],
                        start=(a == 0),
                        stop=(a == 1),
                    )
                early = c == 0 and n < 2
                if early:
                    shifted = keep.tile([P, BANK], F32, name="early%d" % n, tag="early%d" % n, align_bytes=64)
                    nc.vector.tensor_scalar(shifted[:], acc3[:], bias_sb[:, n : n + 1], None, ADD)
                else:
                    shifted = ring3.tile([P, BANK], F32, name="shifted", tag="shifted")
                    nc.scalar.activation(shifted[:], acc3[:], IDENTITY, bias=bias_sb[:, n : n + 1])
                nc.vector.tensor_tensor(score[:, n], acc2[:], shifted[:], MAX)
                nc.sync.dma_start(out[rows, cols], score[:, n])
                if early:
                    quantize_x0(n + 2)
